import numpy as np
import ml_dtypes


def mxq(x, axis, fmt="e4m3"):
    dtype, down = {"e4m3": (ml_dtypes.float8_e4m3fn, 7), "e5m2": (ml_dtypes.float8_e5m2, 14)}[fmt]
    v = np.moveaxis(np.asarray(x, np.float32).astype(ml_dtypes.bfloat16).astype(np.float64), axis, -1)
    blocks = v.reshape(v.shape[:-1] + (-1, 32))
    amax = np.abs(blocks).max(-1, keepdims=True)
    byte = np.maximum(np.where(amax > 0, np.frexp(amax)[1] - 1 + 127, 0) - down, 1)
    scale = np.exp2(byte - 127.0)
    codes = (blocks / scale).astype(np.float32).astype(dtype).astype(np.float64)
    return np.moveaxis((codes * scale).reshape(v.shape), -1, axis)


WIDE = False


def mx_kscale(k):
    if not WIDE:
        return np.ones(k)
    levels = np.array([10, -10, 5, -5, 0])
    if k % 512:
        return np.exp2(np.random.permutation(np.resize(levels, k // 32))).repeat(32)
    a = np.empty((k // 512, 16))
    for p in range(k // 512):
        a[p, :8] = np.random.permutation(np.resize(levels, 8))
        for g in range(8):
            far = levels[np.abs(levels - a[p, g]) >= 10]
            a[p, g + 8] = far[np.random.randint(len(far))]
    return np.exp2(a.ravel()).repeat(32)


def f64(x):
    return np.asarray(x).astype(np.float64)


def striped(idx):
    return np.tile(np.asarray(idx).reshape(-1, 16).T, (8, 1)).astype(np.uint16)


def unstriped(offs):
    return offs[:16].T.reshape(-1).astype(np.int64)


E2M1 = np.array([0.0, 0.5, 1.0, 1.5, 2.0, 3.0, 4.0, 6.0, -0.0, -0.5, -1.0, -1.5, -2.0, -3.0, -4.0, -6.0])


def pack_weight(w, fmt):
    k, n = w.shape
    w = f64(np.asarray(w, np.float32).astype(ml_dtypes.bfloat16)).reshape(k // 32, 32, n)
    amax = np.abs(w).max(1)
    if fmt == "e4m3":
        byte = np.frexp(amax)[1] - 1 + 127 - 7
    else:
        mant, ex = np.frexp(amax / 6.0)
        byte = np.where(mant > 0.5, ex, ex - 1) + 127
    byte = np.clip(np.where(amax > 0, byte, 1), 1, 254)
    scaled = (w * np.exp2(127.0 - byte)[:, None, :]).reshape(k, n).astype(np.float32)
    by_word = np.ascontiguousarray(scaled.reshape(k // 512, 128, 4, n).transpose(0, 1, 3, 2))
    if fmt == "e4m3":
        words = by_word.astype(ml_dtypes.float8_e4m3fn).view(np.uint8)
    else:
        c = by_word.astype(ml_dtypes.float4_e2m1fn).view(np.uint8) & 0xF
        words = (c[..., 0::2] | (c[..., 1::2] << 4)).reshape(k // 512, 128, 2 * n)
    return np.ascontiguousarray(words), np.ascontiguousarray(byte.astype(np.uint8).reshape(k // 512, 16, n))


def unpack_weight(words, scales, fmt):
    g, _, n = scales.shape
    words = np.ascontiguousarray(words).reshape(g, 128, n, -1)
    if fmt == "e4m3":
        vals = words.view(ml_dtypes.float8_e4m3fn).astype(np.float64)
    else:
        nib = np.empty((g, 128, n, 4), np.uint8)
        nib[..., 0::2] = words & 0xF
        nib[..., 1::2] = words >> 4
        vals = E2M1[nib]
    vals = vals * np.repeat(np.exp2(scales.astype(np.float64) - 127.0), 8, axis=1)[..., None]
    return vals.transpose(0, 1, 3, 2).reshape(g * 512, n)


D, E, T, I, Q, G = 512, 512, 2048, 512, 512, 64


def setup_inputs():
    n = np.random.standard_normal
    idx = np.random.permutation(T)[:I]
    fd = mx_kscale(D)
    fe = mx_kscale(E)
    keysp = pack_weight(n((D, T)) / fd[:, None], "e4m3")
    valsp = pack_weight(n((E, T)) / fe[:, None], "e4m3")
    return {
        "query": (n((D, Q)) * 0.5 / np.sqrt(D) * fd[:, None]).astype(np.float32),
        "query2": (n((D, Q)) * 0.5 / np.sqrt(D) * fd[:, None]).astype(np.float32),
        "keys_words": keysp[0],
        "keys_scales": keysp[1],
        "share": (np.random.uniform(0.05, 0.95, (I, 1))).astype(np.float32),
        "lse": (np.random.uniform(6.2, 6.5, (1, Q))).astype(np.float32),
        "gout": (n((E, Q)) * 1 / np.sqrt(E) * fe[:, None]).astype(np.float32),
        "vals_words": valsp[0],
        "vals_scales": valsp[1],
        "delta": (np.random.uniform(-0.3, 0.3, (1, Q))).astype(np.float32),
        "old": (1.0 * n((I, G))).astype(np.float32),
        "offs": striped(idx),
    }


def reference(query, query2, keys_words, keys_scales, share, lse, gout, vals_words, vals_scales, delta, old, offs):
    idx = unstriped(offs)
    keysu = unpack_weight(keys_words, keys_scales, "e4m3")
    valsu = unpack_weight(vals_words, vals_scales, "e4m3")
    keysidxg = keysu[:, idx]
    queryq = mxq(f64(query), 0, "e4m3")
    a = keysidxg.T @ queryq
    query2q = mxq(f64(query2), 0, "e4m3")
    b = keysidxg.T @ query2q
    valsidxg = valsu[:, idx]
    goutq = mxq(f64(gout), 0, "e4m3")
    dp = valsidxg.T @ goutq
    df = a - b
    ds = np.exp(b + df * f64(share) - f64(lse)) * (dp - f64(delta)) * df * 512.0
    y = ds.reshape(I, G, Q // G).sum(axis=2) + f64(old)
    return y

@@ -1,0 +1,195 @@
+from contextlib import ExitStack
+
+import concourse.mybir as mybir
+
+D, E, T, I, Q, G = 512, 512, 2048, 512, 512, 64
+FLOPS = 3 * 2 * D * I * Q
+
+F32 = mybir.dt.float32
+BF16 = mybir.dt.bfloat16
+I32 = mybir.dt.int32
+U32 = mybir.dt.uint32
+U16 = mybir.dt.uint16
+U8 = mybir.dt.uint8
+FP8X4 = mybir.dt.float8_e4m3fn_x4
+ALU = mybir.AluOpType
+ACT = mybir.ActivationFunctionType
+
+P = 128
+PACK = 4
+HALVES = 2
+HQ = Q // HALVES
+TILES = HQ // P
+SLOT_TILES = I // P
+HG = G // HALVES
+LEFT = P // HG
+SCALE = 512.0
+
+
+def tile_attend_gshares_kernel(tc, query, query2, keys_words, keys_scales, share, lse, gout,
+                                vals_words, vals_scales, delta, old, offs, out):
+    nc = tc.nc
+    with ExitStack() as ctx:
+        held = ctx.enter_context(tc.tile_pool(name="held", bufs=1))
+        work = ctx.enter_context(tc.tile_pool(name="work", bufs=2))
+        psum = ctx.enter_context(tc.psum_pool(name="psum", bufs=8))
+
+        offsets = held.tile([P, I // 16], U16, name="offsets")
+        nc.sync.dma_start(offsets[:], offs)
+
+        def load_words(words, name, tag):
+            pool_words = held.tile([P, T], U32, name=name, tag=tag, align_bytes=64)
+            nc.sync.dma_start(pool_words[:].bitcast(I32), words[0].rearrange("p n t -> p (n t)").bitcast(I32))
+            return pool_words
+
+        def load_scales(scales, name, clear):
+            plane = held.tile([P, T], U8, name=name, tag=name, align_bytes=64)
+            clear.memset(plane[:].bitcast(I32), 0)
+            for quad in range(4):
+                nc.sync.dma_start(plane[32 * quad : 32 * quad + 4, :].bitcast(I32),
+                                scales[0, 4 * quad : 4 * quad + 4, :].bitcast(I32))
+            return plane
+
+        def load_half(x, half, name, tag):
+            raw = held.tile([P, PACK, HQ], F32, name=name, tag=tag)
+            nc.sync.dma_start(raw[:], x[:, half * HQ : (half + 1) * HQ].rearrange("(p t) c -> p t c", t=PACK))
+            return raw
+
+        def gather(window, dtype, name):
+            picked = held.tile([P, I], dtype, name=name, align_bytes=64)
+            nc.vector.tensor_copy(picked[:], window[:].indirect(offsets[:]))
+            return picked
+
+        def cast(raw, name, on_scalar, sign):
+            grouped = held.tile([P, TILES, P, PACK], BF16, name=name, align_bytes=64)
+            dst = grouped[:].rearrange("p j m t -> p m j t")
+            src = raw[:].rearrange("p t (m j) -> p m j t", j=TILES)
+            if on_scalar:
+                nc.scalar.activation(dst, src, ACT.Copy, scale=sign)
+            else:
+                nc.vector.tensor_copy(dst, src)
+            return grouped
+
+        def quantize(grouped, name):
+            codes = held.tile([P, HQ], U32, name=name + "_codes", align_bytes=64)
+            scales = held.tile([P, HQ], U8, name=name + "_scales", align_bytes=64)
+            nc.vector.quantize_mx(out=codes[:].bitcast(FP8X4), scales=scales[:],
+                                  in_=grouped[:].rearrange("p j m t -> p (j m t)"))
+            return codes, scales
+
+        def product(bank, rows, j, cols, start, stop):
+            sl = slice(j * P, (j + 1) * P)
+            nc.tensor.matmul_mx(out=bank[:], lhsT=rows[0][:, sl].bitcast(FP8X4), lhsT_scale=rows[1][:, sl],
+                                rhs=cols[0][:].bitcast(FP8X4), rhs_scale=cols[1][:], start=start, stop=stop)
+
+        raw_q2 = load_half(query2, 0, "raw_q2_0", "stage_a")
+        raw_q = load_half(query, 0, "raw_q_0", "stage_b")
+        share_cols = held.tile([P, SLOT_TILES], F32, name="share_cols")
+        nc.sync.dma_start(share_cols[:], share.rearrange("(p t) o -> p (t o)", t=SLOT_TILES))
+        key_plane = load_scales(keys_scales, "key_plane", nc.vector)
+        zeros = held.tile([P, P], F32, name="zeros", tag="key_pool", align_bytes=64)
+        nc.vector.memset(zeros[:], 0.0)
+        ident = held.tile([P, P], F32, name="ident")
+        nc.gpsimd.affine_select(out=ident[:], in_=zeros[:], compare_op=ALU.not_equal, fill=1.0, base=0,
+                                pattern=[[-1, P]], channel_multiplier=1)
+        warm = held.tile([P, 1], F32, name="warm", tag="lse_cols")
+        nc.scalar.activation(warm[:], ident[:, 0:1], ACT.Exp)
+        key_pool = load_words(keys_words, "key_pool", "key_pool")
+        val_plane = load_scales(vals_scales, "val_plane", nc.gpsimd)
+
+        lse_cols = held.tile([P, HALVES, TILES], F32, name="lse_cols", tag="lse_cols")
+        nc.sync.dma_start(lse_cols[:], lse[0].rearrange("(h p j) -> p h j", h=HALVES, j=TILES))
+        nq2_b = [cast(raw_q2, "nq2_b0", True, -1.0)]
+        q_b = [cast(raw_q, "q_b0", False, 1.0)]
+        raw_q2 = load_half(query2, 1, "raw_q2_1", "stage_a")
+        raw_q = load_half(query, 1, "raw_q_1", "stage_b")
+        nq2 = [quantize(nq2_b[0], "nq2_0")]
+        q1 = [quantize(q_b[0], "q_0")]
+        key_bytes = gather(key_plane, U8, "key_bytes")
+        val_pool = load_words(vals_words, "val_pool", "key_plane")
+        keys = (gather(key_pool, U32, "key_words"), key_bytes)
+        val_bytes = gather(val_plane, U8, "val_bytes")
+        delta_cols = held.tile([P, HALVES, TILES], F32, name="delta_cols", tag="val_plane", align_bytes=64)
+        nc.sync.dma_start(delta_cols[:], delta[0].rearrange("(h p j) -> p h j", h=HALVES, j=TILES))
+        old_sb = held.tile([P, SLOT_TILES, G], F32, name="old_sb", tag="key_pool", align_bytes=64)
+        nc.sync.dma_start(old_sb[:], old.rearrange("(t p) g -> p t g", p=P))
+
+        spread = psum.tile([P, SLOT_TILES, P], F32, name="spread", tag="bank")
+        for t in range(SLOT_TILES):
+            nc.tensor.transpose(spread[:, t, :], share_cols[:, t : t + 1].to_broadcast([P, P]), ident[:])
+        share_rows = held.tile([P, P, SLOT_TILES], F32, name="share_rows")
+        nc.scalar.copy(share_rows[:], spread[:].rearrange("p t n -> p n t"))
+        share_row = share_rows[:].rearrange("p n t -> p (n t)")
+        neg_lse = held.tile([P, HALVES * TILES], F32, name="neg_lse")
+        nc.gpsimd.tensor_scalar(neg_lse[:], lse_cols[:].rearrange("p h j -> p (h j)"), -1.0, 0.0, ALU.mult, ALU.add)
+
+        def turn(acc, ds_j, t, j):
+            nc.tensor.matmul(acc, lhsT=ds_j[:, t * P : (t + 1) * P], rhs=ident[:],
+                             is_transpose=True, start=(j == 0), stop=(j == TILES - 1))
+
+        def add_neighbours(dst, acc):
+            nc.vector.tensor_reduce(dst, acc.rearrange("p (g r) -> p g r", r=LEFT), mybir.AxisListType.X, ALU.add)
+
+        weights = {}
+        for half in range(HALVES):
+            if half == 1:
+                nq2.append(quantize(cast(raw_q2, "nq2_b1", True, -1.0), "nq2_1"))
+                q1.append(quantize(cast(raw_q, "q_b1", True, 1.0), "q_1"))
+                raw_g = [load_half(gout, 0, "raw_g_0", "stage_a"), load_half(gout, 1, "raw_g_1", "stage_b")]
+            for j in range(TILES):
+                n = half * TILES + j
+                nb = psum.tile([P, I], F32, name="nb", tag="bank")
+                product(nb, nq2[half], j, keys, True, True)
+                nb_sb = work.tile([P, I], F32, name="nb_sb", bufs=4)
+                nc.scalar.copy(nb_sb[:], nb[:])
+                bank = psum.tile([P, I], F32, name="df", tag="bank")
+                if n == 0:
+                    product(bank, q1[half], j, keys, True, True)
+                    df = work.tile([P, I], F32, name="df_sb")
+                    nc.vector.tensor_tensor(df[:], bank[:], nb_sb[:], ALU.add)
+                else:
+                    product(bank, q1[half], j, keys, True, False)
+                    product(bank, nq2[half], j, keys, False, True)
+                    df = bank
+                mixed = work.tile([P, I], F32, name="mixed", bufs=4)
+                both = nc.gpsimd if n == 0 else nc.vector
+                both.tensor_tensor(mixed[:], df[:], share_row, ALU.mult)
+                score = work.tile([P, I], F32, name="score", bufs=4)
+                nc.gpsimd.tensor_tensor(score[:], mixed[:], nb_sb[:], ALU.subtract)
+                prob = work.tile([P, I], F32, name="prob", bufs=4)
+                nc.scalar.activation(prob[:], score[:], ACT.Exp, bias=neg_lse[:, n : n + 1])
+                w = held.tile([P, I], F32, name="w%d" % n)
+                both.tensor_tensor(w[:], df[:], prob[:], ALU.mult)
+                weights[n] = w
+
+        vals = (gather(val_pool, U32, "val_words"), val_bytes)
+        for half in range(HALVES):
+            g_b = cast(raw_g[half], "g_b%d" % half, half == 0, 1.0)
+            gq = quantize(g_b, "g_%d" % half)
+            ds = []
+            for j in range(TILES):
+                n = half * TILES + j
+                dp = psum.tile([P, I], F32, name="dp", tag="bank")
+                product(dp, gq, j, vals, True, True)
+                ds_j = work.tile([P, I], F32, name="ds", bufs=4)
+                nc.vector.scalar_tensor_tensor(ds_j[:], dp[:], delta_cols[:, half, j : j + 1], weights[n][:],
+                                               ALU.subtract, ALU.mult)
+                ds.append(ds_j)
+            sums = work.tile([P, SLOT_TILES, HG], F32, name="sums")
+            if half == 0:
+                acc = psum.tile([P, SLOT_TILES, P], F32, name="acc", tag="bank")
+                for t in range(SLOT_TILES):
+                    for j in range(TILES):
+                        turn(acc[:, t, :], ds[j], t, j)
+                add_neighbours(sums[:].rearrange("p t g -> p (t g)"), acc[:].rearrange("p t c -> p (t c)"))
+            else:
+                accs = [psum.tile([P, P], F32, name="acc%d" % t, tag="bank") for t in range(SLOT_TILES)]
+                for j in range(TILES):
+                    for t in range(SLOT_TILES):
+                        turn(accs[t][:], ds[j], t, j)
+                for t in range(SLOT_TILES):
+                    add_neighbours(sums[:, t, :], accs[t][:])
+            res = work.tile([P, SLOT_TILES, HG], F32, name="res")
+            gs = slice(half * HG, (half + 1) * HG)
+            nc.vector.scalar_tensor_tensor(res[:], sums[:], SCALE, old_sb[:, :, gs], ALU.mult, ALU.add)
+            nc.sync.dma_start(out.rearrange("(t p) g -> p t g", p=P)[:, :, gs], res[:])

@@ -1,6 +1,7 @@
 from contextlib import ExitStack
 
 import concourse.mybir as mybir
+from concourse.masks import make_identity
 
 D, E, T, I, Q, G = 512, 512, 2048, 512, 512, 64
 FLOPS = 3 * 2 * D * I * Q
@@ -31,43 +32,45 @@ def tile_attend_gshares_kernel(tc, query, query2, keys_words, keys_scales, share
     nc = tc.nc
     with ExitStack() as ctx:
         held = ctx.enter_context(tc.tile_pool(name="held", bufs=1))
-        work = ctx.enter_context(tc.tile_pool(name="work", bufs=2))
         psum = ctx.enter_context(tc.psum_pool(name="psum", bufs=8))
 
         offsets = held.tile([P, I // 16], U16, name="offsets")
         nc.sync.dma_start(offsets[:], offs)
 
-        def load_words(words, name, tag):
-            pool_words = held.tile([P, T], U32, name=name, tag=tag, align_bytes=64)
+        def load_words(words, name):
+            pool_words = held.tile([P, T], U32, name=name, tag=name, align_bytes=64)
             nc.sync.dma_start(pool_words[:].bitcast(I32), words[0].rearrange("p n t -> p (n t)").bitcast(I32))
             return pool_words
 
-        def load_scales(scales, name, clear):
-            plane = held.tile([P, T], U8, name=name, tag=name, align_bytes=64)
-            clear.memset(plane[:].bitcast(I32), 0)
+        def fill_scales(plane, scales):
             for quad in range(4):
-                nc.sync.dma_start(plane[32 * quad : 32 * quad + 4, :].bitcast(I32),
-                                scales[0, 4 * quad : 4 * quad + 4, :].bitcast(I32))
+                nc.scalar.dma_start(plane[32 * quad : 32 * quad + 4, :].bitcast(I32),
+                                    scales[0, 4 * quad : 4 * quad + 4, :].bitcast(I32))
+
+        def load_scales(scales, name):
+            plane = held.tile([P, T], U8, name=name, tag=name, align_bytes=64)
+            nc.gpsimd.memset(plane[:].bitcast(I32), 0)
+            fill_scales(plane, scales)
             return plane
 
-        def load_half(x, half, name, tag):
-            raw = held.tile([P, PACK, HQ], F32, name=name, tag=tag)
+        def load_half(x, half, name):
+            raw = held.tile([P, PACK, HQ], F32, name=name, tag=name, align_bytes=64)
             nc.sync.dma_start(raw[:], x[:, half * HQ : (half + 1) * HQ].rearrange("(p t) c -> p t c", t=PACK))
             return raw
 
-        def gather(window, dtype, name):
-            picked = held.tile([P, I], dtype, name=name, align_bytes=64)
+        def gather(window, dtype, name, tag):
+            picked = held.tile([P, I], dtype, name=name, tag=tag, align_bytes=64)
             nc.vector.tensor_copy(picked[:], window[:].indirect(offsets[:]))
             return picked
 
-        def cast(raw, name, on_scalar, sign):
-            grouped = held.tile([P, TILES, P, PACK], BF16, name=name, align_bytes=64)
-            dst = grouped[:].rearrange("p j m t -> p m j t")
-            src = raw[:].rearrange("p t (m j) -> p m j t", j=TILES)
+        def cast(raw, name, on_scalar, sign, tag):
+            grouped = held.tile([P, TILES, P, PACK], BF16, name=name, tag=tag, align_bytes=64)
+            dst = grouped[:]
+            src = raw[:].rearrange("p t (m j) -> p j m t", j=TILES)
             if on_scalar:
                 nc.scalar.activation(dst, src, ACT.Copy, scale=sign)
             else:
-                nc.vector.tensor_copy(dst, src)
+                nc.vector.tensor_scalar(dst, src, sign, None, ALU.mult)
             return grouped
 
         def quantize(grouped, name):
@@ -82,36 +85,34 @@ def tile_attend_gshares_kernel(tc, query, query2, keys_words, keys_scales, share
             nc.tensor.matmul_mx(out=bank[:], lhsT=rows[0][:, sl].bitcast(FP8X4), lhsT_scale=rows[1][:, sl],
                                 rhs=cols[0][:].bitcast(FP8X4), rhs_scale=cols[1][:], start=start, stop=stop)
 
-        raw_q2 = load_half(query2, 0, "raw_q2_0", "stage_a")
-        raw_q = load_half(query, 0, "raw_q_0", "stage_b")
-        share_cols = held.tile([P, SLOT_TILES], F32, name="share_cols")
-        nc.sync.dma_start(share_cols[:], share.rearrange("(p t) o -> p (t o)", t=SLOT_TILES))
-        key_plane = load_scales(keys_scales, "key_plane", nc.vector)
-        zeros = held.tile([P, P], F32, name="zeros", tag="key_pool", align_bytes=64)
-        nc.vector.memset(zeros[:], 0.0)
-        ident = held.tile([P, P], F32, name="ident")
-        nc.gpsimd.affine_select(out=ident[:], in_=zeros[:], compare_op=ALU.not_equal, fill=1.0, base=0,
-                                pattern=[[-1, P]], channel_multiplier=1)
-        warm = held.tile([P, 1], F32, name="warm", tag="lse_cols")
-        nc.scalar.activation(warm[:], ident[:, 0:1], ACT.Exp)
-        key_pool = load_words(keys_words, "key_pool", "key_pool")
-        val_plane = load_scales(vals_scales, "val_plane", nc.gpsimd)
+        def load_columns(row, name, queue):
+            cols = held.tile([P, HALVES, TILES], F32, name=name)
+            queue.dma_start(cols[:], row[0].rearrange("(h p j) -> p h j", h=HALVES, j=TILES))
+            return cols[:].rearrange("p h j -> p (h j)")
 
-        lse_cols = held.tile([P, HALVES, TILES], F32, name="lse_cols", tag="lse_cols")
-        nc.sync.dma_start(lse_cols[:], lse[0].rearrange("(h p j) -> p h j", h=HALVES, j=TILES))
-        nq2_b = [cast(raw_q2, "nq2_b0", True, -1.0)]
-        q_b = [cast(raw_q, "q_b0", False, 1.0)]
-        raw_q2 = load_half(query2, 1, "raw_q2_1", "stage_a")
-        raw_q = load_half(query, 1, "raw_q_1", "stage_b")
-        nq2 = [quantize(nq2_b[0], "nq2_0")]
-        q1 = [quantize(q_b[0], "q_0")]
-        key_bytes = gather(key_plane, U8, "key_bytes")
-        val_pool = load_words(vals_words, "val_pool", "key_plane")
-        keys = (gather(key_pool, U32, "key_words"), key_bytes)
-        val_bytes = gather(val_plane, U8, "val_bytes")
-        delta_cols = held.tile([P, HALVES, TILES], F32, name="delta_cols", tag="val_plane", align_bytes=64)
-        nc.sync.dma_start(delta_cols[:], delta[0].rearrange("(h p j) -> p h j", h=HALVES, j=TILES))
-        old_sb = held.tile([P, SLOT_TILES, G], F32, name="old_sb", tag="key_pool", align_bytes=64)
+        share_cols = held.tile([P, SLOT_TILES], F32, name="share_cols")
+        nc.scalar.dma_start(share_cols[:], share.rearrange("(p t) o -> p (t o)", t=SLOT_TILES))
+        lse_cols = load_columns(lse, "lse_cols", nc.scalar)
+        key_plane = load_scales(keys_scales, "key_plane")
+        key_pool = load_words(keys_words, "key_pool")
+        raw_q2 = [load_half(query2, 0, "raw_q2_0")]
+        raw_q = [load_half(query, 0, "raw_q_0")]
+        val_plane = held.tile([P, T], U8, name="val_plane", tag="val_plane", align_bytes=64)
+        nc.gpsimd.memset(val_plane[:].bitcast(I32), 0)
+        ident = held.tile([P, P], F32, name="ident")
+        make_identity(nc, ident[:])
+        warm = held.tile([P, 1], F32, name="warm")
+        nc.scalar.activation(warm[:], ident[:, 0:1], ACT.Exp)
+        neg_lse = held.tile([P, HALVES * TILES], F32, name="neg_lse")
+        nc.gpsimd.tensor_scalar(neg_lse[:], lse_cols, -1.0, 0.0, ALU.mult, ALU.add)
+        fill_scales(val_plane, vals_scales)
+        raw_q2.append(load_half(query2, 1, "raw_q2_1"))
+        raw_q.append(load_half(query, 1, "raw_q_1"))
+        val_pool = load_words(vals_words, "val_pool")
+        raw_g = [load_half(gout, 0, "raw_g_0")]
+        delta_cols = load_columns(delta, "delta_cols", nc.sync)
+        raw_g.append(load_half(gout, 1, "raw_g_1"))
+        old_sb = held.tile([P, SLOT_TILES, G], F32, name="old_sb")
         nc.sync.dma_start(old_sb[:], old.rearrange("(t p) g -> p t g", p=P))
 
         spread = psum.tile([P, SLOT_TILES, P], F32, name="spread", tag="bank")
@@ -120,76 +121,112 @@ def tile_attend_gshares_kernel(tc, query, query2, keys_words, keys_scales, share
         share_rows = held.tile([P, P, SLOT_TILES], F32, name="share_rows")
         nc.scalar.copy(share_rows[:], spread[:].rearrange("p t n -> p n t"))
         share_row = share_rows[:].rearrange("p n t -> p (n t)")
-        neg_lse = held.tile([P, HALVES * TILES], F32, name="neg_lse")
-        nc.gpsimd.tensor_scalar(neg_lse[:], lse_cols[:].rearrange("p h j -> p (h j)"), -1.0, 0.0, ALU.mult, ALU.add)
 
-        def turn(acc, ds_j, t, j):
-            nc.tensor.matmul(acc, lhsT=ds_j[:, t * P : (t + 1) * P], rhs=ident[:],
+        key_bytes = gather(key_plane, U8, "key_bytes", "key_bytes")
+        keys = (gather(key_pool, U32, "key_words", "key_plane"), key_bytes)
+        nq2 = quantize(cast(raw_q2[0], "nq2_b0", False, -1.0, "nq2_b0"), "nq2_0")
+        q1 = quantize(cast(raw_q[0], "q_b0", False, 1.0, "q_b0"), "q_0")
+        val_bytes = gather(val_plane, U8, "val_bytes", "val_bytes")
+        nq2_b = cast(raw_q2[1], "nq2_b1", True, -1.0, "nq2_b1")
+        q_b = cast(raw_q[1], "q_b1", True, 1.0, "q_b1")
+
+        def wide(name, tag=None):
+            return held.tile([P, I], F32, name=name, tag=tag or name, align_bytes=64)
+
+        nb, df, mixed, prob, w, ds = {}, {}, {}, {}, {}, {}
+
+        def bank(name):
+            return psum.tile([P, I], F32, name=name, tag="bank")
+
+        def mix(n, tag=None):
+            mixed[n] = wide("mixed%d" % n, tag)
+            nc.vector.tensor_tensor(mixed[n][:], df[n][:], share_row, ALU.mult)
+
+        def weigh(n):
+            score = wide("score%d" % n)
+            nc.vector.tensor_tensor(score[:], mixed[n][:], nb[n][:], ALU.subtract)
+            prob[n] = wide("prob%d" % n)
+            nc.scalar.activation(prob[n][:], score[:], ACT.Exp, bias=neg_lse[:, n : n + 1])
+
+        def times_df(n):
+            w[n] = wide("w%d" % n)
+            nc.vector.tensor_tensor(w[n][:], df[n][:], prob[n][:], ALU.mult)
+
+        def gradient(n, gq):
+            dp = psum.tile([P, I], F32, name="dp%d" % n, tag="bank")
+            product(dp, gq, n % TILES, vals, True, True)
+            ds[n] = wide("ds%d" % n)
+            nc.vector.scalar_tensor_tensor(ds[n][:], dp[:], delta_cols[:, n : n + 1], w[n][:], ALU.subtract, ALU.mult)
+
+        def turn(acc, n, t):
+            j = n % TILES
+            nc.tensor.matmul(acc, lhsT=ds[n][:, t * P : (t + 1) * P], rhs=ident[:],
                              is_transpose=True, start=(j == 0), stop=(j == TILES - 1))
 
-        def add_neighbours(dst, acc):
-            nc.vector.tensor_reduce(dst, acc.rearrange("p (g r) -> p g r", r=LEFT), mybir.AxisListType.X, ALU.add)
+        out_rows = out.rearrange("(t p) g -> p t g", p=P)
 
-        weights = {}
-        for half in range(HALVES):
-            if half == 1:
-                nq2.append(quantize(cast(raw_q2, "nq2_b1", True, -1.0), "nq2_1"))
-                q1.append(quantize(cast(raw_q, "q_b1", True, 1.0), "q_1"))
-                raw_g = [load_half(gout, 0, "raw_g_0", "stage_a"), load_half(gout, 1, "raw_g_1", "stage_b")]
-            for j in range(TILES):
-                n = half * TILES + j
-                nb = psum.tile([P, I], F32, name="nb", tag="bank")
-                product(nb, nq2[half], j, keys, True, True)
-                nb_sb = work.tile([P, I], F32, name="nb_sb", bufs=4)
-                nc.scalar.copy(nb_sb[:], nb[:])
-                bank = psum.tile([P, I], F32, name="df", tag="bank")
-                if n == 0:
-                    product(bank, q1[half], j, keys, True, True)
-                    df = work.tile([P, I], F32, name="df_sb")
-                    nc.vector.tensor_tensor(df[:], bank[:], nb_sb[:], ALU.add)
-                else:
-                    product(bank, q1[half], j, keys, True, False)
-                    product(bank, nq2[half], j, keys, False, True)
-                    df = bank
-                mixed = work.tile([P, I], F32, name="mixed", bufs=4)
-                both = nc.gpsimd if n == 0 else nc.vector
-                both.tensor_tensor(mixed[:], df[:], share_row, ALU.mult)
-                score = work.tile([P, I], F32, name="score", bufs=4)
-                nc.gpsimd.tensor_tensor(score[:], mixed[:], nb_sb[:], ALU.subtract)
-                prob = work.tile([P, I], F32, name="prob", bufs=4)
-                nc.scalar.activation(prob[:], score[:], ACT.Exp, bias=neg_lse[:, n : n + 1])
-                w = held.tile([P, I], F32, name="w%d" % n)
-                both.tensor_tensor(w[:], df[:], prob[:], ALU.mult)
-                weights[n] = w
+        nb_bank = bank("nb0")
+        product(nb_bank, nq2, 0, keys, True, True)
+        nb[0] = wide("nb_sb")
+        nc.scalar.copy(nb[0][:], nb_bank[:])
+        nb[1], df[1], a_bank = bank("nb1"), bank("df1"), bank("a0")
+        product(nb[1], nq2, 1, keys, True, True)
+        product(df[1], nq2, 1, keys, True, False)
+        product(a_bank, q1, 0, keys, True, True)
+        product(df[1], q1, 1, keys, False, True)
+        df[0] = wide("df_sb", "val_plane")
+        nc.vector.tensor_tensor(df[0][:], a_bank[:], nb[0][:], ALU.add)
+        nq2 = quantize(nq2_b, "nq2_1")
+        mix(0)
+        mix(1, "nq2_b1")
+        weigh(0)
+        q1 = quantize(q_b, "q_1")
+        weigh(1)
+        for n in (2, 3):
+            nb[n], df[n] = bank("nb%d" % n), bank("df%d" % n)
+            product(nb[n], nq2, n % TILES, keys, True, True)
+            product(df[n], nq2, n % TILES, keys, True, False)
+        for n in (2, 3):
+            product(df[n], q1, n % TILES, keys, False, True)
+        vals = (gather(val_pool, U32, "val_words", "val_words"), val_bytes)
+        times_df(0)
+        times_df(1)
+        gq = quantize(cast(raw_g[0], "g_b0", True, 1.0, "g_b0"), "g_0")
+        mix(2)
+        mix(3)
+        gradient(0, gq)
+        gradient(1, gq)
+        weigh(2)
+        weigh(3)
 
-        vals = (gather(val_pool, U32, "val_words"), val_bytes)
-        for half in range(HALVES):
-            g_b = cast(raw_g[half], "g_b%d" % half, half == 0, 1.0)
-            gq = quantize(g_b, "g_%d" % half)
-            ds = []
-            for j in range(TILES):
-                n = half * TILES + j
-                dp = psum.tile([P, I], F32, name="dp", tag="bank")
-                product(dp, gq, j, vals, True, True)
-                ds_j = work.tile([P, I], F32, name="ds", bufs=4)
-                nc.vector.scalar_tensor_tensor(ds_j[:], dp[:], delta_cols[:, half, j : j + 1], weights[n][:],
-                                               ALU.subtract, ALU.mult)
-                ds.append(ds_j)
-            sums = work.tile([P, SLOT_TILES, HG], F32, name="sums")
-            if half == 0:
-                acc = psum.tile([P, SLOT_TILES, P], F32, name="acc", tag="bank")
-                for t in range(SLOT_TILES):
-                    for j in range(TILES):
-                        turn(acc[:, t, :], ds[j], t, j)
-                add_neighbours(sums[:].rearrange("p t g -> p (t g)"), acc[:].rearrange("p t c -> p (t c)"))
-            else:
-                accs = [psum.tile([P, P], F32, name="acc%d" % t, tag="bank") for t in range(SLOT_TILES)]
-                for j in range(TILES):
-                    for t in range(SLOT_TILES):
-                        turn(accs[t][:], ds[j], t, j)
-                for t in range(SLOT_TILES):
-                    add_neighbours(sums[:, t, :], accs[t][:])
-            res = work.tile([P, SLOT_TILES, HG], F32, name="res")
-            gs = slice(half * HG, (half + 1) * HG)
-            nc.vector.scalar_tensor_tensor(res[:], sums[:], SCALE, old_sb[:, :, gs], ALU.mult, ALU.add)
-            nc.sync.dma_start(out.rearrange("(t p) g -> p t g", p=P)[:, :, gs], res[:])
+        acc = psum.tile([P, SLOT_TILES, HG, LEFT], F32, name="acc", tag="bank")
+        for t in range(SLOT_TILES):
+            for n in range(TILES):
+                turn(acc[:, t, :, :].rearrange("p g r -> p (g r)"), n, t)
+        parts = held.tile([P, LEFT, SLOT_TILES * HG], F32, name="parts")
+        nc.scalar.activation(parts[:], acc[:].rearrange("p t g r -> p r (t g)"), ACT.Copy, scale=SCALE)
+        pairs = held.tile([P, 2, SLOT_TILES * HG], F32, name="pairs")
+        nc.gpsimd.tensor_tensor(pairs[:], parts[:, 0:2, :], parts[:, 2:4, :], ALU.add)
+        sums = held.tile([P, SLOT_TILES, HG], F32, name="sums0")
+        nc.gpsimd.tensor_tensor(sums[:].rearrange("p t g -> p (t g)"), pairs[:, 0, :], pairs[:, 1, :], ALU.add)
+        res = held.tile([P, SLOT_TILES, HG], F32, name="res0")
+        nc.gpsimd.tensor_tensor(res[:], sums[:], old_sb[:, :, 0:HG], ALU.add)
+        nc.sync.dma_start(out_rows[:, :, 0:HG], res[:])
+
+        gq = quantize(cast(raw_g[1], "g_b1", True, 1.0, "g_b1"), "g_1")
+        times_df(2)
+        times_df(3)
+        gradient(2, gq)
+        accs = [psum.tile([P, P], F32, name="acc%d" % t, tag="bank") for t in range(SLOT_TILES)]
+        for t in range(SLOT_TILES):
+            turn(accs[t][:], 2, t)
+        gradient(3, gq)
+        for t in range(SLOT_TILES):
+            turn(accs[t][:], 3, t)
+        sums = held.tile([P, SLOT_TILES, HG], F32, name="sums1")
+        for t in range(SLOT_TILES):
+            nc.vector.tensor_reduce(sums[:, t, :], accs[t][:].rearrange("p (g r) -> p g r", r=LEFT),
+                                    mybir.AxisListType.X, ALU.add)
+        res = held.tile([P, SLOT_TILES, HG], F32, name="res1")
+        nc.vector.scalar_tensor_tensor(res[:], sums[:], SCALE, old_sb[:, :, HG:G], ALU.mult, ALU.add)
+        nc.sync.dma_start(out_rows[:, :, HG:G], res[:])

@@ -43,9 +43,8 @@ def tile_attend_gshares_kernel(tc, query, query2, keys_words, keys_scales, share
             return pool_words
 
         def fill_scales(plane, scales):
-            for quad in range(4):
-                nc.scalar.dma_start(plane[32 * quad : 32 * quad + 4, :].bitcast(I32),
-                                    scales[0, 4 * quad : 4 * quad + 4, :].bitcast(I32))
+            for r in range(4):
+                nc.sync.dma_start(plane[r:P:32, :].bitcast(I32), scales[0, r:16:4, :].bitcast(I32))
 
         def load_scales(scales, name):
             plane = held.tile([P, T], U8, name=name, tag=name, align_bytes=64)
@@ -65,16 +64,16 @@ def tile_attend_gshares_kernel(tc, query, query2, keys_words, keys_scales, share
 
         def cast(raw, name, on_scalar, sign, tag):
             grouped = held.tile([P, TILES, P, PACK], BF16, name=name, tag=tag, align_bytes=64)
-            dst = grouped[:]
-            src = raw[:].rearrange("p t (m j) -> p j m t", j=TILES)
+            dst = grouped[:].rearrange("p j m t -> p m j t")
+            src = raw[:].rearrange("p t (m j) -> p m j t", j=TILES)
             if on_scalar:
                 nc.scalar.activation(dst, src, ACT.Copy, scale=sign)
             else:
-                nc.vector.tensor_scalar(dst, src, sign, None, ALU.mult)
+                nc.vector.tensor_copy(dst, src)
             return grouped
 
-        def quantize(grouped, name):
-            codes = held.tile([P, HQ], U32, name=name + "_codes", align_bytes=64)
+        def quantize(grouped, name, tag=None):
+            codes = held.tile([P, HQ], U32, name=name + "_codes", tag=tag or name, align_bytes=64)
             scales = held.tile([P, HQ], U8, name=name + "_scales", align_bytes=64)
             nc.vector.quantize_mx(out=codes[:].bitcast(FP8X4), scales=scales[:],
                                   in_=grouped[:].rearrange("p j m t -> p (j m t)"))
@@ -82,7 +81,7 @@ def tile_attend_gshares_kernel(tc, query, query2, keys_words, keys_scales, share
 
         def product(bank, rows, j, cols, start, stop):
             sl = slice(j * P, (j + 1) * P)
-            nc.tensor.matmul_mx(out=bank[:], lhsT=rows[0][:, sl].bitcast(FP8X4), lhsT_scale=rows[1][:, sl],
+            nc.tensor.matmul_mx(out=bank, lhsT=rows[0][:, sl].bitcast(FP8X4), lhsT_scale=rows[1][:, sl],
                                 rhs=cols[0][:].bitcast(FP8X4), rhs_scale=cols[1][:], start=start, stop=stop)
 
         def load_columns(row, name, queue):
@@ -93,25 +92,22 @@ def tile_attend_gshares_kernel(tc, query, query2, keys_words, keys_scales, share
         share_cols = held.tile([P, SLOT_TILES], F32, name="share_cols")
         nc.scalar.dma_start(share_cols[:], share.rearrange("(p t) o -> p (t o)", t=SLOT_TILES))
         lse_cols = load_columns(lse, "lse_cols", nc.scalar)
-        key_plane = load_scales(keys_scales, "key_plane")
         key_pool = load_words(keys_words, "key_pool")
+        key_plane = load_scales(keys_scales, "key_plane")
         raw_q2 = [load_half(query2, 0, "raw_q2_0")]
         raw_q = [load_half(query, 0, "raw_q_0")]
-        val_plane = held.tile([P, T], U8, name="val_plane", tag="val_plane", align_bytes=64)
-        nc.gpsimd.memset(val_plane[:].bitcast(I32), 0)
+        val_plane = load_scales(vals_scales, "val_plane")
         ident = held.tile([P, P], F32, name="ident")
         make_identity(nc, ident[:])
         warm = held.tile([P, 1], F32, name="warm")
         nc.scalar.activation(warm[:], ident[:, 0:1], ACT.Exp)
         neg_lse = held.tile([P, HALVES * TILES], F32, name="neg_lse")
         nc.gpsimd.tensor_scalar(neg_lse[:], lse_cols, -1.0, 0.0, ALU.mult, ALU.add)
-        fill_scales(val_plane, vals_scales)
         raw_q2.append(load_half(query2, 1, "raw_q2_1"))
+        delta_cols = load_columns(delta, "delta_cols", nc.sync)
         raw_q.append(load_half(query, 1, "raw_q_1"))
         val_pool = load_words(vals_words, "val_pool")
-        raw_g = [load_half(gout, 0, "raw_g_0")]
-        delta_cols = load_columns(delta, "delta_cols", nc.sync)
-        raw_g.append(load_half(gout, 1, "raw_g_1"))
+        raw_g = [load_half(gout, half, "raw_g_%d" % half) for half in range(HALVES)]
         old_sb = held.tile([P, SLOT_TILES, G], F32, name="old_sb")
         nc.sync.dma_start(old_sb[:], old.rearrange("(t p) g -> p t g", p=P))
 
@@ -122,111 +118,111 @@ def tile_attend_gshares_kernel(tc, query, query2, keys_words, keys_scales, share
         nc.scalar.copy(share_rows[:], spread[:].rearrange("p t n -> p n t"))
         share_row = share_rows[:].rearrange("p n t -> p (n t)")
 
-        key_bytes = gather(key_plane, U8, "key_bytes", "key_bytes")
-        keys = (gather(key_pool, U32, "key_words", "key_plane"), key_bytes)
-        nq2 = quantize(cast(raw_q2[0], "nq2_b0", False, -1.0, "nq2_b0"), "nq2_0")
-        q1 = quantize(cast(raw_q[0], "q_b0", False, 1.0, "q_b0"), "q_0")
+        keys = (gather(key_pool, U32, "key_words", "key_words"), gather(key_plane, U8, "key_bytes", "key_bytes"))
+        nq2_b = cast(raw_q2[0], "nq2_b0", True, -1.0, "nq2_b0")
+        q_b = cast(raw_q[0], "q_b0", False, 1.0, "q_b0")
+        nq2 = quantize(nq2_b, "nq2_0")
+        q1 = quantize(q_b, "q_0")
         val_bytes = gather(val_plane, U8, "val_bytes", "val_bytes")
         nq2_b = cast(raw_q2[1], "nq2_b1", True, -1.0, "nq2_b1")
-        q_b = cast(raw_q[1], "q_b1", True, 1.0, "q_b1")
 
         def wide(name, tag=None):
-            return held.tile([P, I], F32, name=name, tag=tag or name, align_bytes=64)
+            return held.tile([P, I], F32, name=name, tag=tag or name, align_bytes=64)[:]
 
-        nb, df, mixed, prob, w, ds = {}, {}, {}, {}, {}, {}
+        nb, df, dp, mixed, prob, w, ds = {}, {}, {}, {}, {}, {}, {}
 
         def bank(name):
             return psum.tile([P, I], F32, name=name, tag="bank")
 
-        def mix(n, tag=None):
-            mixed[n] = wide("mixed%d" % n, tag)
-            nc.vector.tensor_tensor(mixed[n][:], df[n][:], share_row, ALU.mult)
+        def mix(n, dst):
+            mixed[n] = dst
+            nc.vector.tensor_tensor(dst, df[n], share_row, ALU.mult)
 
-        def weigh(n):
-            score = wide("score%d" % n)
-            nc.vector.tensor_tensor(score[:], mixed[n][:], nb[n][:], ALU.subtract)
+        def weigh(n, engine, score):
+            engine.tensor_tensor(score, mixed[n], nb[n], ALU.subtract)
             prob[n] = wide("prob%d" % n)
-            nc.scalar.activation(prob[n][:], score[:], ACT.Exp, bias=neg_lse[:, n : n + 1])
+            nc.scalar.activation(prob[n], score, ACT.Exp, bias=neg_lse[:, n : n + 1])
 
-        def times_df(n):
-            w[n] = wide("w%d" % n)
-            nc.vector.tensor_tensor(w[n][:], df[n][:], prob[n][:], ALU.mult)
+        def times_df(n, engine, dst):
+            w[n] = dst
+            engine.tensor_tensor(dst, df[n], prob[n], ALU.mult)
 
-        def gradient(n, gq):
-            dp = psum.tile([P, I], F32, name="dp%d" % n, tag="bank")
-            product(dp, gq, n % TILES, vals, True, True)
-            ds[n] = wide("ds%d" % n)
-            nc.vector.scalar_tensor_tensor(ds[n][:], dp[:], delta_cols[:, n : n + 1], w[n][:], ALU.subtract, ALU.mult)
+        def value_scores(n, gq):
+            dp[n] = bank("dp%d" % n)[:]
+            product(dp[n], gq, n % TILES, vals, True, True)
 
-        def turn(acc, n, t):
-            j = n % TILES
+        def gradient(n, dst):
+            ds[n] = dst
+            nc.vector.scalar_tensor_tensor(ds[n], dp[n], delta_cols[:, n : n + 1], w[n], ALU.subtract, ALU.mult)
+
+        def turn(acc, n, t, first):
             nc.tensor.matmul(acc, lhsT=ds[n][:, t * P : (t + 1) * P], rhs=ident[:],
-                             is_transpose=True, start=(j == 0), stop=(j == TILES - 1))
+                             is_transpose=True, start=first, stop=not first)
 
         out_rows = out.rearrange("(t p) g -> p t g", p=P)
 
         nb_bank = bank("nb0")
-        product(nb_bank, nq2, 0, keys, True, True)
-        nb[0] = wide("nb_sb")
-        nc.scalar.copy(nb[0][:], nb_bank[:])
-        nb[1], df[1], a_bank = bank("nb1"), bank("df1"), bank("a0")
+        product(nb_bank[:], nq2, 0, keys, True, True)
+        nb[0] = wide("nb_sb0", "raw_q2_1")
+        nc.scalar.copy(nb[0], nb_bank[:])
+        a_bank = bank("a0")
+        product(a_bank[:], q1, 0, keys, True, True)
+        nb[1], df[1] = bank("nb1")[:], bank("df1")[:]
         product(nb[1], nq2, 1, keys, True, True)
         product(df[1], nq2, 1, keys, True, False)
-        product(a_bank, q1, 0, keys, True, True)
         product(df[1], q1, 1, keys, False, True)
-        df[0] = wide("df_sb", "val_plane")
-        nc.vector.tensor_tensor(df[0][:], a_bank[:], nb[0][:], ALU.add)
         nq2 = quantize(nq2_b, "nq2_1")
-        mix(0)
-        mix(1, "nq2_b1")
-        weigh(0)
+        df[0] = wide("df_sb")
+        nc.vector.tensor_tensor(df[0], a_bank[:], nb[0], ALU.add)
+        q_b = cast(raw_q[1], "q_b1", True, 1.0, "q_b1")
+        mix(0, wide("mixed0"))
         q1 = quantize(q_b, "q_1")
-        weigh(1)
+        mix(1, wide("mixed1", "q_b1"))
+        weigh(0, nc.vector, wide("score0"))
+        weigh(1, nc.vector, wide("score1"))
         for n in (2, 3):
-            nb[n], df[n] = bank("nb%d" % n), bank("df%d" % n)
+            nb[n], df[n] = bank("nb%d" % n)[:], bank("df%d" % n)[:]
             product(nb[n], nq2, n % TILES, keys, True, True)
             product(df[n], nq2, n % TILES, keys, True, False)
         for n in (2, 3):
             product(df[n], q1, n % TILES, keys, False, True)
         vals = (gather(val_pool, U32, "val_words", "val_words"), val_bytes)
-        times_df(0)
-        times_df(1)
-        gq = quantize(cast(raw_g[0], "g_b0", True, 1.0, "g_b0"), "g_0")
-        mix(2)
-        mix(3)
-        gradient(0, gq)
-        gradient(1, gq)
-        weigh(2)
-        weigh(3)
+        late = held.tile([P, 4, I], F32, name="late", tag="val_pool", align_bytes=64)
+        times_df(0, nc.gpsimd, late[:, 3, :])
+        mix(2, late[:, 1, :])
+        mix(3, late[:, 2, :])
+        gq = quantize(cast(raw_g[0], "g_b0", True, 1.0, "g_b0"), "g_0", "prob0")
+        value_scores(0, gq)
+        value_scores(1, gq)
+        times_df(1, nc.vector, late[:, 0, :])
+        weigh(3, nc.vector, wide("score3", "g_b0"))
+        gq = quantize(cast(raw_g[1], "g_b1", True, 1.0, "g_b1"), "g_1")
+        value_scores(3, gq)
+        value_scores(2, gq)
+        last = held.tile([P, 2, I], F32, name="last", tag="g_b1", align_bytes=64)
+        weigh(2, nc.vector, last[:, 0, :])
+        gradient(0, last[:, 1, :])
+        gradient(1, wide("ds1"))
 
-        acc = psum.tile([P, SLOT_TILES, HG, LEFT], F32, name="acc", tag="bank")
+        acc = psum.tile([P, SLOT_TILES, P], F32, name="acc", tag="bank")
         for t in range(SLOT_TILES):
             for n in range(TILES):
-                turn(acc[:, t, :, :].rearrange("p g r -> p (g r)"), n, t)
-        parts = held.tile([P, LEFT, SLOT_TILES * HG], F32, name="parts")
-        nc.scalar.activation(parts[:], acc[:].rearrange("p t g r -> p r (t g)"), ACT.Copy, scale=SCALE)
-        pairs = held.tile([P, 2, SLOT_TILES * HG], F32, name="pairs")
-        nc.gpsimd.tensor_tensor(pairs[:], parts[:, 0:2, :], parts[:, 2:4, :], ALU.add)
-        sums = held.tile([P, SLOT_TILES, HG], F32, name="sums0")
-        nc.gpsimd.tensor_tensor(sums[:].rearrange("p t g -> p (t g)"), pairs[:, 0, :], pairs[:, 1, :], ALU.add)
-        res = held.tile([P, SLOT_TILES, HG], F32, name="res0")
-        nc.gpsimd.tensor_tensor(res[:], sums[:], old_sb[:, :, 0:HG], ALU.add)
-        nc.sync.dma_start(out_rows[:, :, 0:HG], res[:])
-
-        gq = quantize(cast(raw_g[1], "g_b1", True, 1.0, "g_b1"), "g_1")
-        times_df(2)
-        times_df(3)
-        gradient(2, gq)
+                turn(acc[:, t, :], n, t, n == 0)
+        times_df(3, nc.vector, wide("w3"))
+        times_df(2, nc.vector, wide("w2"))
+        gradient(3, wide("ds3"))
         accs = [psum.tile([P, P], F32, name="acc%d" % t, tag="bank") for t in range(SLOT_TILES)]
         for t in range(SLOT_TILES):
-            turn(accs[t][:], 2, t)
-        gradient(3, gq)
+            turn(accs[t][:], 3, t, True)
+        gradient(2, wide("ds2"))
         for t in range(SLOT_TILES):
-            turn(accs[t][:], 3, t)
-        sums = held.tile([P, SLOT_TILES, HG], F32, name="sums1")
+            turn(accs[t][:], 2, t, False)
+        sums = held.tile([P, SLOT_TILES, G], F32, name="sums", tag="w2", align_bytes=64)
+        nc.vector.tensor_reduce(sums[:, :, 0:HG], acc[:].rearrange("p t (g r) -> p t g r", r=LEFT),
+                                mybir.AxisListType.X, ALU.add)
         for t in range(SLOT_TILES):
-            nc.vector.tensor_reduce(sums[:, t, :], accs[t][:].rearrange("p (g r) -> p g r", r=LEFT),
+            nc.vector.tensor_reduce(sums[:, t, HG:G], accs[t][:].rearrange("p (g r) -> p g r", r=LEFT),
                                     mybir.AxisListType.X, ALU.add)
-        res = held.tile([P, SLOT_TILES, HG], F32, name="res1")
-        nc.vector.scalar_tensor_tensor(res[:], sums[:], SCALE, old_sb[:, :, HG:G], ALU.mult, ALU.add)
-        nc.sync.dma_start(out_rows[:, :, HG:G], res[:])
+        res = held.tile([P, SLOT_TILES, G], F32, name="res")
+        nc.vector.scalar_tensor_tensor(res[:], sums[:], SCALE, old_sb[:], ALU.mult, ALU.add)
+        nc.sync.dma_start(out_rows, res[:])

@@ -4,7 +4,7 @@ import concourse.mybir as mybir
 from concourse.masks import make_identity
 
 D, E, T, I, Q, G = 512, 512, 2048, 512, 512, 64
-FLOPS = 3 * 2 * D * I * Q
+FLOPS = 2 * (2 * D + E) * I * Q
 
 F32 = mybir.dt.float32
 BF16 = mybir.dt.bfloat16
@@ -18,6 +18,7 @@ ACT = mybir.ActivationFunctionType
 
 P = 128
 PACK = 4
+BLOCKS = D // 32
 HALVES = 2
 HQ = Q // HALVES
 TILES = HQ // P
@@ -42,14 +43,11 @@ def tile_attend_gshares_kernel(tc, query, query2, keys_words, keys_scales, share
             nc.sync.dma_start(pool_words[:].bitcast(I32), words[0].rearrange("p n t -> p (n t)").bitcast(I32))
             return pool_words
 
-        def fill_scales(plane, scales):
-            for r in range(4):
-                nc.sync.dma_start(plane[r:P:32, :].bitcast(I32), scales[0, r:16:4, :].bitcast(I32))
-
-        def load_scales(scales, name):
+        def load_plane(scales, name):
             plane = held.tile([P, T], U8, name=name, tag=name, align_bytes=64)
             nc.gpsimd.memset(plane[:].bitcast(I32), 0)
-            fill_scales(plane, scales)
+            for r in range(4):
+                nc.sync.dma_start(plane[r:P:32, :].bitcast(I32), scales[0, r:BLOCKS:4, :].bitcast(I32))
             return plane
 
         def load_half(x, half, name):
@@ -57,57 +55,56 @@ def tile_attend_gshares_kernel(tc, query, query2, keys_words, keys_scales, share
             nc.sync.dma_start(raw[:], x[:, half * HQ : (half + 1) * HQ].rearrange("(p t) c -> p t c", t=PACK))
             return raw
 
-        def gather(window, dtype, name, tag):
-            picked = held.tile([P, I], dtype, name=name, tag=tag, align_bytes=64)
-            nc.vector.tensor_copy(picked[:], window[:].indirect(offsets[:]))
-            return picked
-
-        def cast(raw, name, on_scalar, sign, tag):
-            grouped = held.tile([P, TILES, P, PACK], BF16, name=name, tag=tag, align_bytes=64)
-            dst = grouped[:].rearrange("p j m t -> p m j t")
-            src = raw[:].rearrange("p t (m j) -> p m j t", j=TILES)
-            if on_scalar:
-                nc.scalar.activation(dst, src, ACT.Copy, scale=sign)
-            else:
-                nc.vector.tensor_copy(dst, src)
-            return grouped
-
-        def quantize(grouped, name, tag=None):
-            codes = held.tile([P, HQ], U32, name=name + "_codes", tag=tag or name, align_bytes=64)
-            scales = held.tile([P, HQ], U8, name=name + "_scales", align_bytes=64)
-            nc.vector.quantize_mx(out=codes[:].bitcast(FP8X4), scales=scales[:],
-                                  in_=grouped[:].rearrange("p j m t -> p (j m t)"))
-            return codes, scales
-
-        def product(bank, rows, j, cols, start, stop):
-            sl = slice(j * P, (j + 1) * P)
-            nc.tensor.matmul_mx(out=bank, lhsT=rows[0][:, sl].bitcast(FP8X4), lhsT_scale=rows[1][:, sl],
-                                rhs=cols[0][:].bitcast(FP8X4), rhs_scale=cols[1][:], start=start, stop=stop)
-
         def load_columns(row, name, queue):
             cols = held.tile([P, HALVES, TILES], F32, name=name)
             queue.dma_start(cols[:], row[0].rearrange("(h p j) -> p h j", h=HALVES, j=TILES))
             return cols[:].rearrange("p h j -> p (h j)")
 
+        def gather(window, dtype, name):
+            picked = held.tile([P, I], dtype, name=name, tag=name, align_bytes=64)
+            nc.vector.tensor_copy(picked[:], window[:].indirect(offsets[:]))
+            return picked
+
+        def staged(name, count):
+            return held.tile([P, count, TILES, P, PACK], BF16, name=name, tag=name, align_bytes=64)
+
+        def dealt(raw, grouped):
+            return grouped.rearrange("p j m t -> p m j t"), raw[:].rearrange("p t (m j) -> p m j t", j=TILES)
+
+        def cast_on_scalar(raw, grouped, sign):
+            dst, src = dealt(raw, grouped)
+            nc.scalar.activation(dst, src, ACT.Copy, scale=sign)
+
+        def quantize(grouped, name, tag=None):
+            width = grouped.shape[1] * HQ
+            codes = held.tile([P, width], U32, name=name + "_codes", tag=tag or name + "_codes", align_bytes=64)
+            scales = held.tile([P, width], U8, name=name + "_scales", align_bytes=64)
+            nc.vector.quantize_mx(out=codes[:].bitcast(FP8X4), scales=scales[:],
+                                  in_=grouped[:].rearrange("p c j m t -> p (c j m t)"))
+            return codes, scales
+
+        def product(acc, rows, j, cols, start, stop):
+            sl = slice(j * P, (j + 1) * P)
+            nc.tensor.matmul_mx(out=acc, lhsT=rows[0][:, sl].bitcast(FP8X4), lhsT_scale=rows[1][:, sl],
+                                rhs=cols[0][:].bitcast(FP8X4), rhs_scale=cols[1][:], start=start, stop=stop)
+
         share_cols = held.tile([P, SLOT_TILES], F32, name="share_cols")
         nc.scalar.dma_start(share_cols[:], share.rearrange("(p t) o -> p (t o)", t=SLOT_TILES))
         lse_cols = load_columns(lse, "lse_cols", nc.scalar)
         key_pool = load_words(keys_words, "key_pool")
-        key_plane = load_scales(keys_scales, "key_plane")
+        key_plane = load_plane(keys_scales, "key_plane")
         raw_q2 = [load_half(query2, 0, "raw_q2_0")]
         raw_q = [load_half(query, 0, "raw_q_0")]
-        val_plane = load_scales(vals_scales, "val_plane")
+        val_plane = load_plane(vals_scales, "val_plane")
         ident = held.tile([P, P], F32, name="ident")
         make_identity(nc, ident[:])
-        warm = held.tile([P, 1], F32, name="warm")
-        nc.scalar.activation(warm[:], ident[:, 0:1], ACT.Exp)
         neg_lse = held.tile([P, HALVES * TILES], F32, name="neg_lse")
         nc.gpsimd.tensor_scalar(neg_lse[:], lse_cols, -1.0, 0.0, ALU.mult, ALU.add)
         raw_q2.append(load_half(query2, 1, "raw_q2_1"))
-        delta_cols = load_columns(delta, "delta_cols", nc.sync)
         raw_q.append(load_half(query, 1, "raw_q_1"))
         val_pool = load_words(vals_words, "val_pool")
         raw_g = [load_half(gout, half, "raw_g_%d" % half) for half in range(HALVES)]
+        delta_cols = load_columns(delta, "delta_cols", nc.sync)
         old_sb = held.tile([P, SLOT_TILES, G], F32, name="old_sb")
         nc.sync.dma_start(old_sb[:], old.rearrange("(t p) g -> p t g", p=P))
 
@@ -115,114 +112,120 @@ def tile_attend_gshares_kernel(tc, query, query2, keys_words, keys_scales, share
         for t in range(SLOT_TILES):
             nc.tensor.transpose(spread[:, t, :], share_cols[:, t : t + 1].to_broadcast([P, P]), ident[:])
         share_rows = held.tile([P, P, SLOT_TILES], F32, name="share_rows")
-        nc.scalar.copy(share_rows[:], spread[:].rearrange("p t n -> p n t"))
-        share_row = share_rows[:].rearrange("p n t -> p (n t)")
+        nc.scalar.activation(share_rows[:], spread[:].rearrange("p t m -> p m t"), ACT.Copy)
+        share_row = share_rows[:].rearrange("p m t -> p (m t)")
 
-        keys = (gather(key_pool, U32, "key_words", "key_words"), gather(key_plane, U8, "key_bytes", "key_bytes"))
-        nq2_b = cast(raw_q2[0], "nq2_b0", True, -1.0, "nq2_b0")
-        q_b = cast(raw_q[0], "q_b0", False, 1.0, "q_b0")
-        nq2 = quantize(nq2_b, "nq2_0")
-        q1 = quantize(q_b, "q_0")
-        val_bytes = gather(val_plane, U8, "val_bytes", "val_bytes")
-        nq2_b = cast(raw_q2[1], "nq2_b1", True, -1.0, "nq2_b1")
+        keys = (gather(key_pool, U32, "key_words"), gather(key_plane, U8, "key_bytes"))
+        first_b = staged("first_b", 2)
+        cast_on_scalar(raw_q2[0], first_b[:, 0, :, :, :], -1.0)
+        nc.vector.tensor_copy(*dealt(raw_q[0], first_b[:, 1, :, :, :]))
+        first = quantize(first_b, "first")
+        val_bytes = gather(val_plane, U8, "val_bytes")
+        nq2_b = staged("nq2_b", 1)
+        cast_on_scalar(raw_q2[1], nq2_b[:, 0, :, :, :], -1.0)
 
         def wide(name, tag=None):
             return held.tile([P, I], F32, name=name, tag=tag or name, align_bytes=64)[:]
 
+        def bank(name):
+            return psum.tile([P, I], F32, name=name, tag="bank")[:]
+
         nb, df, dp, mixed, prob, w, ds = {}, {}, {}, {}, {}, {}, {}
 
-        def bank(name):
-            return psum.tile([P, I], F32, name=name, tag="bank")
-
-        def mix(n, dst):
+        def mix(n, engine, dst):
             mixed[n] = dst
-            nc.vector.tensor_tensor(dst, df[n], share_row, ALU.mult)
+            engine.tensor_tensor(dst, df[n], share_row, ALU.mult)
 
-        def weigh(n, engine, score):
-            engine.tensor_tensor(score, mixed[n], nb[n], ALU.subtract)
+        def weigh(n):
+            score = wide("score%d" % n)
+            nc.vector.tensor_tensor(score, mixed[n], nb[n], ALU.subtract)
             prob[n] = wide("prob%d" % n)
             nc.scalar.activation(prob[n], score, ACT.Exp, bias=neg_lse[:, n : n + 1])
 
-        def times_df(n, engine, dst):
-            w[n] = dst
-            engine.tensor_tensor(dst, df[n], prob[n], ALU.mult)
+        def times_df(n, engine, tag=None):
+            w[n] = wide("w%d" % n, tag)
+            engine.tensor_tensor(w[n], df[n], prob[n], ALU.mult)
 
         def value_scores(n, gq):
-            dp[n] = bank("dp%d" % n)[:]
+            dp[n] = bank("dp%d" % n)
             product(dp[n], gq, n % TILES, vals, True, True)
 
-        def gradient(n, dst):
-            ds[n] = dst
+        def gradient(n):
+            ds[n] = wide("ds%d" % n)
             nc.vector.scalar_tensor_tensor(ds[n], dp[n], delta_cols[:, n : n + 1], w[n], ALU.subtract, ALU.mult)
 
-        def turn(acc, n, t, first):
+        def turn(acc, n, t):
             nc.tensor.matmul(acc, lhsT=ds[n][:, t * P : (t + 1) * P], rhs=ident[:],
-                             is_transpose=True, start=first, stop=not first)
+                             is_transpose=True, start=(n % TILES == 0), stop=(n % TILES == TILES - 1))
 
-        out_rows = out.rearrange("(t p) g -> p t g", p=P)
-
-        nb_bank = bank("nb0")
-        product(nb_bank[:], nq2, 0, keys, True, True)
-        nb[0] = wide("nb_sb0", "raw_q2_1")
-        nc.scalar.copy(nb[0], nb_bank[:])
-        a_bank = bank("a0")
-        product(a_bank[:], q1, 0, keys, True, True)
-        nb[1], df[1] = bank("nb1")[:], bank("df1")[:]
-        product(nb[1], nq2, 1, keys, True, True)
-        product(df[1], nq2, 1, keys, True, False)
-        product(df[1], q1, 1, keys, False, True)
-        nq2 = quantize(nq2_b, "nq2_1")
-        df[0] = wide("df_sb")
-        nc.vector.tensor_tensor(df[0], a_bank[:], nb[0], ALU.add)
-        q_b = cast(raw_q[1], "q_b1", True, 1.0, "q_b1")
-        mix(0, wide("mixed0"))
-        q1 = quantize(q_b, "q_1")
-        mix(1, wide("mixed1", "q_b1"))
-        weigh(0, nc.vector, wide("score0"))
-        weigh(1, nc.vector, wide("score1"))
+        df[0], nb[0] = bank("df0"), bank("nb0")
+        product(df[0], first, 0, keys, True, False)
+        product(df[0], first, TILES, keys, False, True)
+        product(nb[0], first, 0, keys, True, True)
+        nb_bank, a_bank = bank("nb1"), bank("a1")
+        product(nb_bank, first, 1, keys, True, True)
+        product(a_bank, first, TILES + 1, keys, True, True)
+        q_b = staged("q_b", 1)
+        cast_on_scalar(raw_q[1], q_b[:, 0, :, :, :], 1.0)
+        nb[1] = wide("nb_sb", "raw_q_1")
+        nc.scalar.copy(nb[1], nb_bank)
+        nq2 = quantize(nq2_b, "nq2")
+        mix(0, nc.vector, wide("mixed0", "nq2_b"))
+        q1 = quantize(q_b, "q1")
+        weigh(0)
+        df[1] = wide("df_sb")
+        nc.vector.tensor_tensor(df[1], a_bank, nb[1], ALU.add)
         for n in (2, 3):
-            nb[n], df[n] = bank("nb%d" % n)[:], bank("df%d" % n)[:]
+            nb[n], df[n] = bank("nb%d" % n), bank("df%d" % n)
             product(nb[n], nq2, n % TILES, keys, True, True)
             product(df[n], nq2, n % TILES, keys, True, False)
         for n in (2, 3):
             product(df[n], q1, n % TILES, keys, False, True)
-        vals = (gather(val_pool, U32, "val_words", "val_words"), val_bytes)
-        late = held.tile([P, 4, I], F32, name="late", tag="val_pool", align_bytes=64)
-        times_df(0, nc.gpsimd, late[:, 3, :])
-        mix(2, late[:, 1, :])
-        mix(3, late[:, 2, :])
-        gq = quantize(cast(raw_g[0], "g_b0", True, 1.0, "g_b0"), "g_0", "prob0")
-        value_scores(0, gq)
-        value_scores(1, gq)
-        times_df(1, nc.vector, late[:, 0, :])
-        weigh(3, nc.vector, wide("score3", "g_b0"))
-        gq = quantize(cast(raw_g[1], "g_b1", True, 1.0, "g_b1"), "g_1")
-        value_scores(3, gq)
-        value_scores(2, gq)
-        last = held.tile([P, 2, I], F32, name="last", tag="g_b1", align_bytes=64)
-        weigh(2, nc.vector, last[:, 0, :])
-        gradient(0, last[:, 1, :])
-        gradient(1, wide("ds1"))
 
-        acc = psum.tile([P, SLOT_TILES, P], F32, name="acc", tag="bank")
+        vals = (gather(val_pool, U32, "val_words"), val_bytes)
+        late_mixed = held.tile([P, 3, I], F32, name="late_mixed", tag="val_pool", align_bytes=64)
+        mix(1, nc.gpsimd, late_mixed[:, 0, :])
+        times_df(0, nc.vector)
+        mix(2, nc.vector, late_mixed[:, 1, :])
+        mix(3, nc.vector, late_mixed[:, 2, :])
+        g0_b = staged("g0_b", 1)
+        cast_on_scalar(raw_g[0], g0_b[:, 0, :, :, :], 1.0)
+        weigh(1)
+        g0 = quantize(g0_b, "g0", "raw_q_1")
+        value_scores(0, g0)
+        value_scores(1, g0)
+        weigh(2)
+        g1_b = staged("g1_b", 1)
+        cast_on_scalar(raw_g[1], g1_b[:, 0, :, :, :], 1.0)
+        g1 = quantize(g1_b, "g1")
+        value_scores(2, g1)
+        value_scores(3, g1)
+        weigh(3)
+        times_df(1, nc.gpsimd, "g1_b")
+        gradient(0)
+        times_df(2, nc.vector)
+        gradient(1)
+
+        acc_first = psum.tile([P, SLOT_TILES, P], F32, name="acc_first", tag="bank")
         for t in range(SLOT_TILES):
             for n in range(TILES):
-                turn(acc[:, t, :], n, t, n == 0)
-        times_df(3, nc.vector, wide("w3"))
-        times_df(2, nc.vector, wide("w2"))
-        gradient(3, wide("ds3"))
-        accs = [psum.tile([P, P], F32, name="acc%d" % t, tag="bank") for t in range(SLOT_TILES)]
+                turn(acc_first[:, t, :], n, t)
+
+        times_df(3, nc.vector)
+        gradient(2)
+        acc_second = [psum.tile([P, P], F32, name="acc_second%d" % t, tag="bank") for t in range(SLOT_TILES)]
         for t in range(SLOT_TILES):
-            turn(accs[t][:], 3, t, True)
-        gradient(2, wide("ds2"))
+            turn(acc_second[t][:], 2, t)
+        gradient(3)
         for t in range(SLOT_TILES):
-            turn(accs[t][:], 2, t, False)
-        sums = held.tile([P, SLOT_TILES, G], F32, name="sums", tag="w2", align_bytes=64)
-        nc.vector.tensor_reduce(sums[:, :, 0:HG], acc[:].rearrange("p t (g r) -> p t g r", r=LEFT),
+            turn(acc_second[t][:], 3, t)
+
+        sums = held.tile([P, SLOT_TILES, G], F32, name="sums", tag="w3", align_bytes=64)
+        nc.vector.tensor_reduce(sums[:, :, 0:HG], acc_first[:].rearrange("p t (g r) -> p t g r", r=LEFT),
                                 mybir.AxisListType.X, ALU.add)
         for t in range(SLOT_TILES):
-            nc.vector.tensor_reduce(sums[:, t, HG:G], accs[t][:].rearrange("p (g r) -> p g r", r=LEFT),
+            nc.vector.tensor_reduce(sums[:, t, HG:G], acc_second[t][:].rearrange("p (g r) -> p g r", r=LEFT),
                                     mybir.AxisListType.X, ALU.add)
         res = held.tile([P, SLOT_TILES, G], F32, name="res")
         nc.vector.scalar_tensor_tensor(res[:], sums[:], SCALE, old_sb[:], ALU.mult, ALU.add)
-        nc.sync.dma_start(out_rows, res[:])
+        nc.sync.dma_start(out.rearrange("(t p) g -> p t g", p=P), res[:])

from contextlib import ExitStack

import concourse.mybir as mybir
from concourse.masks import make_identity

D, E, T, I, Q, G = 512, 512, 2048, 512, 512, 64
FLOPS = 2 * (2 * D + E) * I * Q

F32 = mybir.dt.float32
BF16 = mybir.dt.bfloat16
I32 = mybir.dt.int32
U32 = mybir.dt.uint32
U16 = mybir.dt.uint16
U8 = mybir.dt.uint8
FP8X4 = mybir.dt.float8_e4m3fn_x4
ALU = mybir.AluOpType
ACT = mybir.ActivationFunctionType

P = 128
PACK = 4
BLOCKS = D // 32
HALVES = 2
HQ = Q // HALVES
TILES = HQ // P
SLOT_TILES = I // P
HG = G // HALVES
LEFT = P // HG
SCALE = 512.0


def tile_attend_gshares_kernel(tc, query, query2, keys_words, keys_scales, share, lse, gout,
                                vals_words, vals_scales, delta, old, offs, out):
    nc = tc.nc
    with ExitStack() as ctx:
        held = ctx.enter_context(tc.tile_pool(name="held", bufs=1))
        psum = ctx.enter_context(tc.psum_pool(name="psum", bufs=8))

        offsets = held.tile([P, I // 16], U16, name="offsets")
        nc.sync.dma_start(offsets[:], offs)

        def load_words(words, name):
            pool_words = held.tile([P, T], U32, name=name, tag=name, align_bytes=64)
            nc.sync.dma_start(pool_words[:].bitcast(I32), words[0].rearrange("p n t -> p (n t)").bitcast(I32))
            return pool_words

        def load_plane(scales, name):
            plane = held.tile([P, T], U8, name=name, tag=name, align_bytes=64)
            nc.gpsimd.memset(plane[:].bitcast(I32), 0)
            for r in range(4):
                nc.sync.dma_start(plane[r:P:32, :].bitcast(I32), scales[0, r:BLOCKS:4, :].bitcast(I32))
            return plane

        def load_half(x, half, name):
            raw = held.tile([P, PACK, HQ], F32, name=name, tag=name, align_bytes=64)
            nc.sync.dma_start(raw[:], x[:, half * HQ : (half + 1) * HQ].rearrange("(p t) c -> p t c", t=PACK))
            return raw

        def load_columns(row, name, queue):
            cols = held.tile([P, HALVES, TILES], F32, name=name)
            queue.dma_start(cols[:], row[0].rearrange("(h p j) -> p h j", h=HALVES, j=TILES))
            return cols[:].rearrange("p h j -> p (h j)")

        def gather(window, dtype, name):
            picked = held.tile([P, I], dtype, name=name, tag=name, align_bytes=64)
            nc.vector.tensor_copy(picked[:], window[:].indirect(offsets[:]))
            return picked

        def staged(name, count):
            return held.tile([P, count, TILES, P, PACK], BF16, name=name, tag=name, align_bytes=64)

        def dealt(raw, grouped):
            return grouped.rearrange("p j m t -> p m j t"), raw[:].rearrange("p t (m j) -> p m j t", j=TILES)

        def cast_on_scalar(raw, grouped, sign):
            dst, src = dealt(raw, grouped)
            nc.scalar.activation(dst, src, ACT.Copy, scale=sign)

        def quantize(grouped, name, tag=None):
            width = grouped.shape[1] * HQ
            codes = held.tile([P, width], U32, name=name + "_codes", tag=tag or name + "_codes", align_bytes=64)
            scales = held.tile([P, width], U8, name=name + "_scales", align_bytes=64)
            nc.vector.quantize_mx(out=codes[:].bitcast(FP8X4), scales=scales[:],
                                  in_=grouped[:].rearrange("p c j m t -> p (c j m t)"))
            return codes, scales

        def product(acc, rows, j, cols, start, stop):
            sl = slice(j * P, (j + 1) * P)
            nc.tensor.matmul_mx(out=acc, lhsT=rows[0][:, sl].bitcast(FP8X4), lhsT_scale=rows[1][:, sl],
                                rhs=cols[0][:].bitcast(FP8X4), rhs_scale=cols[1][:], start=start, stop=stop)

        share_cols = held.tile([P, SLOT_TILES], F32, name="share_cols")
        nc.scalar.dma_start(share_cols[:], share.rearrange("(p t) o -> p (t o)", t=SLOT_TILES))
        lse_cols = load_columns(lse, "lse_cols", nc.scalar)
        key_pool = load_words(keys_words, "key_pool")
        key_plane = load_plane(keys_scales, "key_plane")
        raw_q2 = [load_half(query2, 0, "raw_q2_0")]
        raw_q = [load_half(query, 0, "raw_q_0")]
        val_plane = load_plane(vals_scales, "val_plane")
        ident = held.tile([P, P], F32, name="ident")
        make_identity(nc, ident[:])
        neg_lse = held.tile([P, HALVES * TILES], F32, name="neg_lse")
        nc.gpsimd.tensor_scalar(neg_lse[:], lse_cols, -1.0, 0.0, ALU.mult, ALU.add)
        raw_q2.append(load_half(query2, 1, "raw_q2_1"))
        raw_q.append(load_half(query, 1, "raw_q_1"))
        val_pool = load_words(vals_words, "val_pool")
        raw_g = [load_half(gout, half, "raw_g_%d" % half) for half in range(HALVES)]
        delta_cols = load_columns(delta, "delta_cols", nc.sync)
        old_sb = held.tile([P, SLOT_TILES, G], F32, name="old_sb")
        nc.sync.dma_start(old_sb[:], old.rearrange("(t p) g -> p t g", p=P))

        spread = psum.tile([P, SLOT_TILES, P], F32, name="spread", tag="bank")
        for t in range(SLOT_TILES):
            nc.tensor.transpose(spread[:, t, :], share_cols[:, t : t + 1].to_broadcast([P, P]), ident[:])
        share_rows = held.tile([P, P, SLOT_TILES], F32, name="share_rows")
        nc.scalar.activation(share_rows[:], spread[:].rearrange("p t m -> p m t"), ACT.Copy)
        share_row = share_rows[:].rearrange("p m t -> p (m t)")

        keys = (gather(key_pool, U32, "key_words"), gather(key_plane, U8, "key_bytes"))
        first_b = staged("first_b", 2)
        cast_on_scalar(raw_q2[0], first_b[:, 0, :, :, :], -1.0)
        nc.vector.tensor_copy(*dealt(raw_q[0], first_b[:, 1, :, :, :]))
        first = quantize(first_b, "first")
        val_bytes = gather(val_plane, U8, "val_bytes")
        nq2_b = staged("nq2_b", 1)
        cast_on_scalar(raw_q2[1], nq2_b[:, 0, :, :, :], -1.0)

        def wide(name, tag=None):
            return held.tile([P, I], F32, name=name, tag=tag or name, align_bytes=64)[:]

        def bank(name):
            return psum.tile([P, I], F32, name=name, tag="bank")[:]

        nb, df, dp, mixed, prob, w, ds = {}, {}, {}, {}, {}, {}, {}

        def mix(n, engine, dst):
            mixed[n] = dst
            engine.tensor_tensor(dst, df[n], share_row, ALU.mult)

        def weigh(n):
            score = wide("score%d" % n)
            nc.vector.tensor_tensor(score, mixed[n], nb[n], ALU.subtract)
            prob[n] = wide("prob%d" % n)
            nc.scalar.activation(prob[n], score, ACT.Exp, bias=neg_lse[:, n : n + 1])

        def times_df(n, engine, tag=None):
            w[n] = wide("w%d" % n, tag)
            engine.tensor_tensor(w[n], df[n], prob[n], ALU.mult)

        def value_scores(n, gq):
            dp[n] = bank("dp%d" % n)
            product(dp[n], gq, n % TILES, vals, True, True)

        def gradient(n):
            ds[n] = wide("ds%d" % n)
            nc.vector.scalar_tensor_tensor(ds[n], dp[n], delta_cols[:, n : n + 1], w[n], ALU.subtract, ALU.mult)

        def turn(acc, n, t):
            nc.tensor.matmul(acc, lhsT=ds[n][:, t * P : (t + 1) * P], rhs=ident[:],
                             is_transpose=True, start=(n % TILES == 0), stop=(n % TILES == TILES - 1))

        df[0], nb[0] = bank("df0"), bank("nb0")
        product(df[0], first, 0, keys, True, False)
        product(df[0], first, TILES, keys, False, True)
        product(nb[0], first, 0, keys, True, True)
        nb_bank, a_bank = bank("nb1"), bank("a1")
        product(nb_bank, first, 1, keys, True, True)
        product(a_bank, first, TILES + 1, keys, True, True)
        q_b = staged("q_b", 1)
        cast_on_scalar(raw_q[1], q_b[:, 0, :, :, :], 1.0)
        nb[1] = wide("nb_sb", "raw_q_1")
        nc.scalar.copy(nb[1], nb_bank)
        nq2 = quantize(nq2_b, "nq2")
        mix(0, nc.vector, wide("mixed0", "nq2_b"))
        q1 = quantize(q_b, "q1")
        weigh(0)
        df[1] = wide("df_sb")
        nc.vector.tensor_tensor(df[1], a_bank, nb[1], ALU.add)
        for n in (2, 3):
            nb[n], df[n] = bank("nb%d" % n), bank("df%d" % n)
            product(nb[n], nq2, n % TILES, keys, True, True)
            product(df[n], nq2, n % TILES, keys, True, False)
        for n in (2, 3):
            product(df[n], q1, n % TILES, keys, False, True)

        vals = (gather(val_pool, U32, "val_words"), val_bytes)
        late_mixed = held.tile([P, 3, I], F32, name="late_mixed", tag="val_pool", align_bytes=64)
        mix(1, nc.gpsimd, late_mixed[:, 0, :])
        times_df(0, nc.vector)
        mix(2, nc.vector, late_mixed[:, 1, :])
        mix(3, nc.vector, late_mixed[:, 2, :])
        g0_b = staged("g0_b", 1)
        cast_on_scalar(raw_g[0], g0_b[:, 0, :, :, :], 1.0)
        weigh(1)
        g0 = quantize(g0_b, "g0", "raw_q_1")
        value_scores(0, g0)
        value_scores(1, g0)
        weigh(2)
        g1_b = staged("g1_b", 1)
        cast_on_scalar(raw_g[1], g1_b[:, 0, :, :, :], 1.0)
        g1 = quantize(g1_b, "g1")
        value_scores(2, g1)
        value_scores(3, g1)
        weigh(3)
        times_df(1, nc.gpsimd, "g1_b")
        gradient(0)
        times_df(2, nc.vector)
        gradient(1)

        acc_first = psum.tile([P, SLOT_TILES, P], F32, name="acc_first", tag="bank")
        for t in range(SLOT_TILES):
            for n in range(TILES):
                turn(acc_first[:, t, :], n, t)

        times_df(3, nc.vector)
        gradient(2)
        acc_second = [psum.tile([P, P], F32, name="acc_second%d" % t, tag="bank") for t in range(SLOT_TILES)]
        for t in range(SLOT_TILES):
            turn(acc_second[t][:], 2, t)
        gradient(3)
        for t in range(SLOT_TILES):
            turn(acc_second[t][:], 3, t)

        sums = held.tile([P, SLOT_TILES, G], F32, name="sums", tag="w3", align_bytes=64)
        nc.vector.tensor_reduce(sums[:, :, 0:HG], acc_first[:].rearrange("p t (g r) -> p t g r", r=LEFT),
                                mybir.AxisListType.X, ALU.add)
        for t in range(SLOT_TILES):
            nc.vector.tensor_reduce(sums[:, t, HG:G], acc_second[t][:].rearrange("p (g r) -> p g r", r=LEFT),
                                    mybir.AxisListType.X, ALU.add)
        res = held.tile([P, SLOT_TILES, G], F32, name="res")
        nc.vector.scalar_tensor_tensor(res[:], sums[:], SCALE, old_sb[:], ALU.mult, ALU.add)
        nc.sync.dma_start(out.rearrange("(t p) g -> p t g", p=P), res[:])
